import numpy as np
import ml_dtypes


def mxq(x, axis, fmt="e4m3"):
    dtype, down = {"e4m3": (ml_dtypes.float8_e4m3fn, 7), "e5m2": (ml_dtypes.float8_e5m2, 14)}[fmt]
    v = np.moveaxis(np.asarray(x, np.float32).astype(ml_dtypes.bfloat16).astype(np.float64), axis, -1)
    blocks = v.reshape(v.shape[:-1] + (-1, 32))
    amax = np.abs(blocks).max(-1, keepdims=True)
    byte = np.maximum(np.where(amax > 0, np.frexp(amax)[1] - 1 + 127, 0) - down, 1)
    scale = np.exp2(byte - 127.0)
    codes = (blocks / scale).astype(np.float32).astype(dtype).astype(np.float64)
    return np.moveaxis((codes * scale).reshape(v.shape), -1, axis)


WIDE = False


def mx_kscale(k):
    if not WIDE:
        return np.ones(k)
    levels = np.array([10, -10, 5, -5, 0])
    if k % 512:
        return np.exp2(np.random.permutation(np.resize(levels, k // 32))).repeat(32)
    a = np.empty((k // 512, 16))
    for p in range(k // 512):
        a[p, :8] = np.random.permutation(np.resize(levels, 8))
        for g in range(8):
            far = levels[np.abs(levels - a[p, g]) >= 10]
            a[p, g + 8] = far[np.random.randint(len(far))]
    return np.exp2(a.ravel()).repeat(32)


def f64(x):
    return np.asarray(x).astype(np.float64)


def striped(idx):
    return np.tile(np.asarray(idx).reshape(-1, 16).T, (8, 1)).astype(np.uint16)


def unstriped(offs):
    return offs[:16].T.reshape(-1).astype(np.int64)


E2M1 = np.array([0.0, 0.5, 1.0, 1.5, 2.0, 3.0, 4.0, 6.0, -0.0, -0.5, -1.0, -1.5, -2.0, -3.0, -4.0, -6.0])


def pack_weight(w, fmt):
    k, n = w.shape
    w = f64(np.asarray(w, np.float32).astype(ml_dtypes.bfloat16)).reshape(k // 32, 32, n)
    amax = np.abs(w).max(1)
    if fmt == "e4m3":
        byte = np.frexp(amax)[1] - 1 + 127 - 7
    else:
        mant, ex = np.frexp(amax / 6.0)
        byte = np.where(mant > 0.5, ex, ex - 1) + 127
    byte = np.clip(np.where(amax > 0, byte, 1), 1, 254)
    scaled = (w * np.exp2(127.0 - byte)[:, None, :]).reshape(k, n).astype(np.float32)
    by_word = np.ascontiguousarray(scaled.reshape(k // 512, 128, 4, n).transpose(0, 1, 3, 2))
    if fmt == "e4m3":
        words = by_word.astype(ml_dtypes.float8_e4m3fn).view(np.uint8)
    else:
        c = by_word.astype(ml_dtypes.float4_e2m1fn).view(np.uint8) & 0xF
        words = (c[..., 0::2] | (c[..., 1::2] << 4)).reshape(k // 512, 128, 2 * n)
    return np.ascontiguousarray(words), np.ascontiguousarray(byte.astype(np.uint8).reshape(k // 512, 16, n))


def unpack_weight(words, scales, fmt):
    g, _, n = scales.shape
    words = np.ascontiguousarray(words).reshape(g, 128, n, -1)
    if fmt == "e4m3":
        vals = words.view(ml_dtypes.float8_e4m3fn).astype(np.float64)
    else:
        nib = np.empty((g, 128, n, 4), np.uint8)
        nib[..., 0::2] = words & 0xF
        nib[..., 1::2] = words >> 4
        vals = E2M1[nib]
    vals = vals * np.repeat(np.exp2(scales.astype(np.float64) - 127.0), 8, axis=1)[..., None]
    return vals.transpose(0, 1, 3, 2).reshape(g * 512, n)


def sigmoid(v):
    return 1.0 / (1.0 + np.exp(-v))


D, T, I, Q, Z, M = 512, 2048, 512, 128, 1024, 2048


def setup_inputs():
    n = np.random.standard_normal
    idx = np.random.permutation(T)[:I]
    idx2 = np.random.permutation(Z)[:I]
    idx3 = np.random.permutation(Z)[:I]
    idx4 = np.random.permutation(M)[:I]
    fd = mx_kscale(D)
    keysp = pack_weight(n((D, T)) / fd[:, None], "e2m1")
    return {
        "query": (n((D, Q)) * 1.0 / np.sqrt(D) * fd[:, None]).astype(np.float32),
        "keys_words": keysp[0],
        "keys_scales": keysp[1],
        "old": (np.random.uniform(0.0, 2.0, (Q, M))).astype(np.float32),
        "fade": (np.random.uniform(0.3, 0.9, (Q, 1))).astype(np.float32),
        "offs": striped(idx),
        "offs2": striped(idx2),
        "offs3": striped(idx3),
        "offs4": striped(idx4),
    }


def reference(query, keys_words, keys_scales, old, fade, offs, offs2, offs3, offs4):
    idx = unstriped(offs)
    idx2 = unstriped(offs2)
    idx3 = unstriped(offs3)
    idx4 = unstriped(offs4)
    keysu = unpack_weight(keys_words, keys_scales, "e2m1")
    queryq = mxq(f64(query), 0, "e4m3")
    keysidxg = keysu[:, idx]
    a = queryq.T @ keysidxg
    f0 = np.zeros((Q, Z))
    f0[:, idx2] = a
    s = a + f0[:, idx3]
    w = sigmoid(s)
    ws = w * 2.0
    wf = np.zeros((Q, M))
    wf[:, idx4] = ws
    y = f64(old) * f64(fade) + wf
    return y

@@ -1,0 +1,143 @@
+from contextlib import ExitStack
+
+import concourse.mybir as mybir
+
+D, T, I, Q, Z, M = 512, 2048, 512, 128, 1024, 2048
+FLOPS = 2 * D * I * Q
+
+F32 = mybir.dt.float32
+BF16 = mybir.dt.bfloat16
+I32 = mybir.dt.int32
+U32 = mybir.dt.uint32
+U16 = mybir.dt.uint16
+U8 = mybir.dt.uint8
+FP8X4 = mybir.dt.float8_e4m3fn_x4
+FP4X4 = mybir.dt.float4_e2m1fn_x4
+ADD = mybir.AluOpType.add
+MULT = mybir.AluOpType.mult
+COPY = mybir.ActivationFunctionType.Copy
+SIGMOID = mybir.ActivationFunctionType.Sigmoid
+
+P = 128
+PACK = 4
+HALF = I // 2
+PER_COLUMN = 16
+STORE_WIDTHS = (256, 512, 512, 512, 256)
+
+
+def entries(list_tile, first, last):
+    return list_tile[:, first // PER_COLUMN : last // PER_COLUMN]
+
+
+def tile_attend_passedthrough_counts_lean_kernel(
+    tc, query, keys_words, keys_scales, old, fade, offs, offs2, offs3, offs4, out
+):
+    nc = tc.nc
+    with ExitStack() as ctx:
+        keep = ctx.enter_context(tc.tile_pool(name="keep", bufs=1))
+        psum = ctx.enter_context(tc.psum_pool(name="psum", bufs=1))
+
+        token_list = keep.tile([P, I // PER_COLUMN], U16, name="token_list")
+        put_list = keep.tile([P, I // PER_COLUMN], U16, name="put_list")
+        fetch_list = keep.tile([P, I // PER_COLUMN], U16, name="fetch_list")
+        column_list = keep.tile([P, I // PER_COLUMN], U16, name="column_list")
+
+        pool_scales = keep.tile([P, T], U8, name="pool_scales")
+        pool_words = keep.tile([P, T], U16, name="pool_words")
+        places = keep.tile([P, Z], F32, name="places")
+        new_counts = keep.tile([P, M], F32, name="new_counts")
+        query_raw = keep.tile([P, PACK, Q], F32, name="query_raw", tag="second_scales", align_bytes=64)
+
+        nc.vector.memset(pool_scales[:].bitcast(I32), 0)
+        nc.sync.dma_start(token_list[:], offs)
+        for quad in range(4):
+            nc.sync.dma_start(
+                pool_scales[32 * quad : 32 * quad + 4, :].bitcast(I32),
+                keys_scales[0, 4 * quad : 4 * quad + 4, :].bitcast(I32),
+            )
+        nc.sync.dma_start(put_list[:], offs2)
+        nc.sync.dma_start(pool_words[:].bitcast(I32), keys_words[0].bitcast(I32))
+        nc.sync.dma_start(query_raw[:], query.rearrange("(p j) q -> p j q", j=PACK))
+        nc.sync.dma_start(fetch_list[:], offs3)
+        nc.sync.dma_start(column_list[:], offs4)
+        nc.vector.memset(places[:], 0.0)
+        nc.vector.memset(new_counts[:], 0.0)
+
+        query_bf16 = keep.tile([P, Q, PACK], BF16, name="query_bf16", tag="second_words", align_bytes=64)
+        query_codes = keep.tile([P, Q], U32, name="query_codes", align_bytes=64)
+        query_scales = keep.tile([P, Q], U8, name="query_scales", align_bytes=64)
+        nc.scalar.activation(query_bf16[:], query_raw[:].rearrange("p j q -> p q j"), COPY)
+        nc.vector.quantize_mx(
+            out=query_codes[:].bitcast(FP8X4),
+            scales=query_scales[:],
+            in_=query_bf16[:].rearrange("p q j -> p (q j)"),
+        )
+
+        products = []
+        for half in range(2):
+            first, last = half * HALF, (half + 1) * HALF
+            which = ("first", "second")[half]
+            words = keep.tile([P, HALF], U16, name="slot_words%d" % half, tag=which + "_words", align_bytes=64)
+            scales = keep.tile([P, HALF], U8, name="slot_scales%d" % half, tag=which + "_scales", align_bytes=64)
+            nc.vector.tensor_copy(words[:], pool_words[:].indirect(entries(token_list, first, last)))
+            nc.vector.tensor_copy(scales[:], pool_scales[:].indirect(entries(token_list, first, last)))
+            bank = psum.tile([P, HALF], F32, name="bank%d" % half)
+            nc.tensor.matmul_mx(
+                out=bank[:],
+                lhsT=query_codes[:].bitcast(FP8X4),
+                lhsT_scale=query_scales[:],
+                rhs=words[:].bitcast(FP4X4),
+                rhs_scale=scales[:],
+                start=True,
+                stop=True,
+            )
+            product = keep.tile([P, HALF], F32, name="product%d" % half)
+            target = places[:].indirect(entries(put_list, first, last))
+            if half == 0:
+                nc.scalar.copy(product[:], bank[:])
+                nc.scalar.activation(target, product[:], COPY)
+            else:
+                nc.vector.tensor_copy(product[:], bank[:])
+                nc.vector.tensor_copy(target, product[:])
+            products.append(product)
+
+        old_counts = keep.tile([P, M], F32, name="old_counts", tag="first_words", align_bytes=64)
+        fading = keep.tile([P, 1], F32, name="fading", tag="first_scales", align_bytes=64)
+        nc.sync.dma_start(old_counts[:], old)
+        nc.sync.dma_start(fading[:], fade)
+
+        scores = keep.tile([P, I], F32, name="scores")
+
+        def score(first, last):
+            half, start = divmod(first, HALF)
+            nc.vector.tensor_tensor(
+                scores[:, first:last],
+                places[:].indirect(entries(fetch_list, first, last)),
+                products[half][:, start : start + last - first],
+                ADD,
+            )
+
+        lead = keep.tile([P, HALF], F32, name="lead", tag="weights")
+        for first, last in ((0, 128), (128, 256)):
+            score(first, last)
+            nc.scalar.activation(lead[:, first:last], scores[:, first:last], SIGMOID)
+        nc.scalar.activation(
+            new_counts[:].indirect(entries(column_list, 0, HALF)), lead[:], COPY, scale=2.0
+        )
+        for first, last, tag in ((256, 320, "bridge"), (320, 512, "weights")):
+            score(first, last)
+            weights = keep.tile([P, last - first], F32, name="weights%d" % first, tag=tag)
+            nc.scalar.activation(weights[:], scores[:, first:last], SIGMOID)
+            nc.vector.tensor_tensor(
+                new_counts[:].indirect(entries(column_list, first, last)), weights[:], weights[:], ADD
+            )
+
+        start = 0
+        for number, width in enumerate(STORE_WIDTHS):
+            cols = slice(start, start + width)
+            result = keep.tile([P, width], F32, name="result%d" % number)
+            nc.vector.scalar_tensor_tensor(
+                result[:], old_counts[:, cols], fading[:], new_counts[:, cols], MULT, ADD
+            )
+            nc.sync.dma_start(out[:, cols], result[:])
+            start = start + width

@@ -16,13 +16,16 @@ FP4X4 = mybir.dt.float4_e2m1fn_x4
 ADD = mybir.AluOpType.add
 MULT = mybir.AluOpType.mult
 COPY = mybir.ActivationFunctionType.Copy
-SIGMOID = mybir.ActivationFunctionType.Sigmoid
+TANH = mybir.ActivationFunctionType.Tanh
 
 P = 128
 PACK = 4
 HALF = I // 2
 PER_COLUMN = 16
-STORE_WIDTHS = (256, 512, 512, 512, 256)
+STORE_WIDTHS = (128, 384, 512, 512, 384, 128)
+CAST_SPLIT = 64
+LEAD = 128
+FUSED = 288
 
 
 def entries(list_tile, first, last):
@@ -51,7 +54,7 @@ def tile_attend_passedthrough_counts_lean_kernel(
         nc.vector.memset(pool_scales[:].bitcast(I32), 0)
         nc.sync.dma_start(token_list[:], offs)
         for quad in range(4):
-            nc.sync.dma_start(
+            nc.scalar.dma_start(
                 pool_scales[32 * quad : 32 * quad + 4, :].bitcast(I32),
                 keys_scales[0, 4 * quad : 4 * quad + 4, :].bitcast(I32),
             )
@@ -60,24 +63,28 @@ def tile_attend_passedthrough_counts_lean_kernel(
         nc.sync.dma_start(query_raw[:], query.rearrange("(p j) q -> p j q", j=PACK))
         nc.sync.dma_start(fetch_list[:], offs3)
         nc.sync.dma_start(column_list[:], offs4)
-        nc.vector.memset(places[:], 0.0)
-        nc.vector.memset(new_counts[:], 0.0)
+        ones = keep.tile([P, I - LEAD], F32, name="ones")
+        nc.vector.memset(places[:].bitcast(I32), 0)
+        nc.vector.memset(new_counts[:].bitcast(I32), 0)
+        nc.vector.memset(ones[:], 1.0)
 
-        query_bf16 = keep.tile([P, Q, PACK], BF16, name="query_bf16", tag="second_words", align_bytes=64)
+        query_bf16 = keep.tile([P, Q, PACK], BF16, name="query_bf16", align_bytes=64)
         query_codes = keep.tile([P, Q], U32, name="query_codes", align_bytes=64)
         query_scales = keep.tile([P, Q], U8, name="query_scales", align_bytes=64)
-        nc.scalar.activation(query_bf16[:], query_raw[:].rearrange("p j q -> p q j"), COPY)
+        interleaved = query_raw[:].rearrange("p j q -> p q j")
+        nc.scalar.activation(query_bf16[:, :CAST_SPLIT, :], interleaved[:, :CAST_SPLIT, :], COPY)
+        nc.vector.tensor_copy(query_bf16[:, CAST_SPLIT:, :], interleaved[:, CAST_SPLIT:, :])
         nc.vector.quantize_mx(
             out=query_codes[:].bitcast(FP8X4),
             scales=query_scales[:],
             in_=query_bf16[:].rearrange("p q j -> p (q j)"),
         )
 
-        products = []
+        products = keep.tile([P, I], F32, name="products")
         for half in range(2):
             first, last = half * HALF, (half + 1) * HALF
             which = ("first", "second")[half]
-            words = keep.tile([P, HALF], U16, name="slot_words%d" % half, tag=which + "_words", align_bytes=64)
+            words = keep.tile([P, HALF], U16, name="slot_words%d" % half, tag="slot_words", align_bytes=64)
             scales = keep.tile([P, HALF], U8, name="slot_scales%d" % half, tag=which + "_scales", align_bytes=64)
             nc.vector.tensor_copy(words[:], pool_words[:].indirect(entries(token_list, first, last)))
             nc.vector.tensor_copy(scales[:], pool_scales[:].indirect(entries(token_list, first, last)))
@@ -91,45 +98,39 @@ def tile_attend_passedthrough_counts_lean_kernel(
                 start=True,
                 stop=True,
             )
-            product = keep.tile([P, HALF], F32, name="product%d" % half)
+            product = products[:, first:last]
             target = places[:].indirect(entries(put_list, first, last))
             if half == 0:
-                nc.scalar.copy(product[:], bank[:])
-                nc.scalar.activation(target, product[:], COPY)
+                nc.scalar.copy(product, bank[:])
+                nc.scalar.activation(target, product, COPY)
             else:
-                nc.vector.tensor_copy(product[:], bank[:])
-                nc.vector.tensor_copy(target, product[:])
-            products.append(product)
+                nc.vector.tensor_copy(product, bank[:])
+                nc.vector.tensor_copy(target, product)
 
-        old_counts = keep.tile([P, M], F32, name="old_counts", tag="first_words", align_bytes=64)
+        old_counts = keep.tile([P, M], F32, name="old_counts", tag="slot_words", align_bytes=64)
         fading = keep.tile([P, 1], F32, name="fading", tag="first_scales", align_bytes=64)
         nc.sync.dma_start(old_counts[:], old)
         nc.sync.dma_start(fading[:], fade)
 
         scores = keep.tile([P, I], F32, name="scores")
-
-        def score(first, last):
-            half, start = divmod(first, HALF)
+        fetched = keep.tile([P, I - FUSED], F32, name="fetched")
+        centred = keep.tile([P, I], F32, name="centred")
+        nc.scalar.activation(fetched[:], places[:].indirect(entries(fetch_list, FUSED, I)), COPY)
+        for first, last in ((0, LEAD), (LEAD, FUSED)):
             nc.vector.tensor_tensor(
                 scores[:, first:last],
                 places[:].indirect(entries(fetch_list, first, last)),
-                products[half][:, start : start + last - first],
+                products[:, first:last],
                 ADD,
             )
-
-        lead = keep.tile([P, HALF], F32, name="lead", tag="weights")
-        for first, last in ((0, 128), (128, 256)):
-            score(first, last)
-            nc.scalar.activation(lead[:, first:last], scores[:, first:last], SIGMOID)
-        nc.scalar.activation(
-            new_counts[:].indirect(entries(column_list, 0, HALF)), lead[:], COPY, scale=2.0
-        )
-        for first, last, tag in ((256, 320, "bridge"), (320, 512, "weights")):
-            score(first, last)
-            weights = keep.tile([P, last - first], F32, name="weights%d" % first, tag=tag)
-            nc.scalar.activation(weights[:], scores[:, first:last], SIGMOID)
+        nc.vector.tensor_tensor(scores[:, FUSED:], fetched[:], products[:, FUSED:], ADD)
+        for first, last in ((0, LEAD), (LEAD, I)):
+            nc.scalar.activation(centred[:, first:last], scores[:, first:last], TANH, scale=0.5)
             nc.vector.tensor_tensor(
-                new_counts[:].indirect(entries(column_list, first, last)), weights[:], weights[:], ADD
+                new_counts[:].indirect(entries(column_list, first, last)),
+                centred[:, first:last],
+                ones[:, : last - first],
+                ADD,
             )
 
         start = 0
@@ -139,5 +140,5 @@ def tile_attend_passedthrough_counts_lean_kernel(
             nc.vector.scalar_tensor_tensor(
                 result[:], old_counts[:, cols], fading[:], new_counts[:, cols], MULT, ADD
             )
-            nc.sync.dma_start(out[:, cols], result[:])
+            (nc.sync, nc.scalar)[number % 2].dma_start(out[:, cols], result[:])
             start = start + width

from contextlib import ExitStack

import concourse.mybir as mybir

D, T, I, Q, Z, M = 512, 2048, 512, 128, 1024, 2048
FLOPS = 2 * D * I * Q

F32 = mybir.dt.float32
BF16 = mybir.dt.bfloat16
I32 = mybir.dt.int32
U32 = mybir.dt.uint32
U16 = mybir.dt.uint16
U8 = mybir.dt.uint8
FP8X4 = mybir.dt.float8_e4m3fn_x4
FP4X4 = mybir.dt.float4_e2m1fn_x4
ADD = mybir.AluOpType.add
MULT = mybir.AluOpType.mult
COPY = mybir.ActivationFunctionType.Copy
TANH = mybir.ActivationFunctionType.Tanh

P = 128
PACK = 4
HALF = I // 2
PER_COLUMN = 16
STORE_WIDTHS = (128, 384, 512, 512, 384, 128)
CAST_SPLIT = 64
LEAD = 128
FUSED = 288


def entries(list_tile, first, last):
    return list_tile[:, first // PER_COLUMN : last // PER_COLUMN]


def tile_attend_passedthrough_counts_lean_kernel(
    tc, query, keys_words, keys_scales, old, fade, offs, offs2, offs3, offs4, out
):
    nc = tc.nc
    with ExitStack() as ctx:
        keep = ctx.enter_context(tc.tile_pool(name="keep", bufs=1))
        psum = ctx.enter_context(tc.psum_pool(name="psum", bufs=1))

        token_list = keep.tile([P, I // PER_COLUMN], U16, name="token_list")
        put_list = keep.tile([P, I // PER_COLUMN], U16, name="put_list")
        fetch_list = keep.tile([P, I // PER_COLUMN], U16, name="fetch_list")
        column_list = keep.tile([P, I // PER_COLUMN], U16, name="column_list")

        pool_scales = keep.tile([P, T], U8, name="pool_scales")
        pool_words = keep.tile([P, T], U16, name="pool_words")
        places = keep.tile([P, Z], F32, name="places")
        new_counts = keep.tile([P, M], F32, name="new_counts")
        query_raw = keep.tile([P, PACK, Q], F32, name="query_raw", tag="second_scales", align_bytes=64)

        nc.vector.memset(pool_scales[:].bitcast(I32), 0)
        nc.sync.dma_start(token_list[:], offs)
        for quad in range(4):
            nc.scalar.dma_start(
                pool_scales[32 * quad : 32 * quad + 4, :].bitcast(I32),
                keys_scales[0, 4 * quad : 4 * quad + 4, :].bitcast(I32),
            )
        nc.sync.dma_start(put_list[:], offs2)
        nc.sync.dma_start(pool_words[:].bitcast(I32), keys_words[0].bitcast(I32))
        nc.sync.dma_start(query_raw[:], query.rearrange("(p j) q -> p j q", j=PACK))
        nc.sync.dma_start(fetch_list[:], offs3)
        nc.sync.dma_start(column_list[:], offs4)
        ones = keep.tile([P, I - LEAD], F32, name="ones")
        nc.vector.memset(places[:].bitcast(I32), 0)
        nc.vector.memset(new_counts[:].bitcast(I32), 0)
        nc.vector.memset(ones[:], 1.0)

        query_bf16 = keep.tile([P, Q, PACK], BF16, name="query_bf16", align_bytes=64)
        query_codes = keep.tile([P, Q], U32, name="query_codes", align_bytes=64)
        query_scales = keep.tile([P, Q], U8, name="query_scales", align_bytes=64)
        interleaved = query_raw[:].rearrange("p j q -> p q j")
        nc.scalar.activation(query_bf16[:, :CAST_SPLIT, :], interleaved[:, :CAST_SPLIT, :], COPY)
        nc.vector.tensor_copy(query_bf16[:, CAST_SPLIT:, :], interleaved[:, CAST_SPLIT:, :])
        nc.vector.quantize_mx(
            out=query_codes[:].bitcast(FP8X4),
            scales=query_scales[:],
            in_=query_bf16[:].rearrange("p q j -> p (q j)"),
        )

        products = keep.tile([P, I], F32, name="products")
        for half in range(2):
            first, last = half * HALF, (half + 1) * HALF
            which = ("first", "second")[half]
            words = keep.tile([P, HALF], U16, name="slot_words%d" % half, tag="slot_words", align_bytes=64)
            scales = keep.tile([P, HALF], U8, name="slot_scales%d" % half, tag=which + "_scales", align_bytes=64)
            nc.vector.tensor_copy(words[:], pool_words[:].indirect(entries(token_list, first, last)))
            nc.vector.tensor_copy(scales[:], pool_scales[:].indirect(entries(token_list, first, last)))
            bank = psum.tile([P, HALF], F32, name="bank%d" % half)
            nc.tensor.matmul_mx(
                out=bank[:],
                lhsT=query_codes[:].bitcast(FP8X4),
                lhsT_scale=query_scales[:],
                rhs=words[:].bitcast(FP4X4),
                rhs_scale=scales[:],
                start=True,
                stop=True,
            )
            product = products[:, first:last]
            target = places[:].indirect(entries(put_list, first, last))
            if half == 0:
                nc.scalar.copy(product, bank[:])
                nc.scalar.activation(target, product, COPY)
            else:
                nc.vector.tensor_copy(product, bank[:])
                nc.vector.tensor_copy(target, product)

        old_counts = keep.tile([P, M], F32, name="old_counts", tag="slot_words", align_bytes=64)
        fading = keep.tile([P, 1], F32, name="fading", tag="first_scales", align_bytes=64)
        nc.sync.dma_start(old_counts[:], old)
        nc.sync.dma_start(fading[:], fade)

        scores = keep.tile([P, I], F32, name="scores")
        fetched = keep.tile([P, I - FUSED], F32, name="fetched")
        centred = keep.tile([P, I], F32, name="centred")
        nc.scalar.activation(fetched[:], places[:].indirect(entries(fetch_list, FUSED, I)), COPY)
        for first, last in ((0, LEAD), (LEAD, FUSED)):
            nc.vector.tensor_tensor(
                scores[:, first:last],
                places[:].indirect(entries(fetch_list, first, last)),
                products[:, first:last],
                ADD,
            )
        nc.vector.tensor_tensor(scores[:, FUSED:], fetched[:], products[:, FUSED:], ADD)
        for first, last in ((0, LEAD), (LEAD, I)):
            nc.scalar.activation(centred[:, first:last], scores[:, first:last], TANH, scale=0.5)
            nc.vector.tensor_tensor(
                new_counts[:].indirect(entries(column_list, first, last)),
                centred[:, first:last],
                ones[:, : last - first],
                ADD,
            )

        start = 0
        for number, width in enumerate(STORE_WIDTHS):
            cols = slice(start, start + width)
            result = keep.tile([P, width], F32, name="result%d" % number)
            nc.vector.scalar_tensor_tensor(
                result[:], old_counts[:, cols], fading[:], new_counts[:, cols], MULT, ADD
            )
            (nc.sync, nc.scalar)[number % 2].dma_start(out[:, cols], result[:])
            start = start + width
